import numpy as np
import ml_dtypes


def mxq(x, axis, fmt="e4m3"):
    dtype, down = {"e4m3": (ml_dtypes.float8_e4m3fn, 7), "e5m2": (ml_dtypes.float8_e5m2, 14)}[fmt]
    v = np.moveaxis(np.asarray(x, np.float32).astype(ml_dtypes.bfloat16).astype(np.float64), axis, -1)
    blocks = v.reshape(v.shape[:-1] + (-1, 32))
    amax = np.abs(blocks).max(-1, keepdims=True)
    byte = np.maximum(np.where(amax > 0, np.frexp(amax)[1] - 1 + 127, 0) - down, 1)
    scale = np.exp2(byte - 127.0)
    codes = (blocks / scale).astype(np.float32).astype(dtype).astype(np.float64)
    return np.moveaxis((codes * scale).reshape(v.shape), -1, axis)


WIDE = False


def mx_kscale(k, group=512):
    if not WIDE:
        return np.ones(k)
    levels = np.array([10, -10, 5, -5, 0])
    if group != 512:
        return np.exp2(np.random.permutation(np.resize(levels, k // group))).repeat(group)
    if k % 512:
        return np.exp2(np.random.permutation(np.resize(levels, k // 32))).repeat(32)
    a = np.empty((k // 512, 16))
    for p in range(k // 512):
        a[p, :8] = np.random.permutation(np.resize(levels, 8))
        for g in range(8):
            far = levels[np.abs(levels - a[p, g]) >= 10]
            a[p, g + 8] = far[np.random.randint(len(far))]
    return np.exp2(a.ravel()).repeat(32)


def f64(x):
    return np.asarray(x).astype(np.float64)


G, D, K, M, N = 4, 256, 512, 128, 512


def setup_inputs():
    n = np.random.standard_normal
    s = mx_kscale(D, 0)[:, None]
    u = mx_kscale(K)[:, None]
    return {
        "x": (n((G, D, N)) * s).astype(np.float32),
        "w1": (n((G, D, K)) / np.sqrt(D) / s).astype(np.float32),
        "hs": (np.random.uniform(0.5, 2.0, (G, K, 1)) * u).astype(np.float32),
        "w2": (n((G, K, M)) / np.sqrt(K) / u).astype(np.float32),
        "r": n((G, M, N)).astype(np.float32),
    }


def reference(x, w1, hs, w2, r):
    xq = mxq(f64(x), 1, "e4m3")
    h = mxq(f64(w1), 1, "e4m3").transpose(0, 2, 1) @ xq
    h = (1.0 / (1.0 + np.exp(-(h)))) * f64(hs)
    y = mxq(f64(w2), 1, "e4m3").transpose(0, 2, 1) @ mxq(h, 1, "e4m3")
    y = y + f64(r)
    return y

@@ -1,0 +1,270 @@
+from contextlib import ExitStack
+
+import concourse.mybir as mybir
+
+G, D, K, M, N = 4, 256, 512, 128, 512
+FLOPS = 2 * G * N * (D * K + K * M)
+
+F32 = mybir.dt.float32
+BF16 = mybir.dt.bfloat16
+U32 = mybir.dt.uint32
+U8 = mybir.dt.uint8
+FP8X4 = mybir.dt.float8_e4m3fn_x4
+SIGMOID = mybir.ActivationFunctionType.Sigmoid
+MULT = mybir.AluOpType.mult
+ADD = mybir.AluOpType.add
+
+P = 128
+PACK = 4
+ROWS = 64
+CHUNK = 128
+CHUNKS = N // CHUNK
+Z_BANKS = 3
+
+
+def tile_rows_gmlp_sigmoid_res_kernel(tc, x, w1, hs, w2, r, out):
+    nc = tc.nc
+    with ExitStack() as ctx:
+        sb = ctx.enter_context(tc.tile_pool(name="sb", bufs=1))
+        ps = ctx.enter_context(tc.psum_pool(name="ps", bufs=1))
+        ctx.enter_context(tc.manual_schedule())
+
+        def sbuf(name, shape, dtype):
+            return sb.tile(shape, dtype, name=name, align_bytes=64)
+
+        z_banks = [[ps.tile([P, PACK, CHUNK], F32, name="z%d_%d" % (c, i)) for i in range(Z_BANKS)] for c in range(2)]
+        y_banks = [ps.tile([P, 2, 2 * CHUNK], F32, name="y%d" % i) for i in range(2)]
+
+        def copy(engine, dst, src):
+            if engine == "vector":
+                nc.vector.tensor_copy(out=dst, in_=src)
+            else:
+                nc.scalar.copy(out=dst, in_=src)
+
+        def quantize(name, values):
+            words = values.shape[1] // PACK
+            codes = sbuf(name + "_codes", [P, words], U32)
+            scales = sbuf(name + "_scales", [P, words], U8)
+            nc.vector.quantize_mx(out=codes[:].bitcast(FP8X4), scales=scales[:], in_=values)
+            return codes, scales
+
+        x_raw, w1_raw, w2_raw, r_sb = {}, {}, {}, {}
+        w1_bf, w2_bf, x_bf, h_bf, sig, res = {}, {}, {}, {}, {}, {}
+        w1_q, w2_q, x_q, h_q = {}, {}, {}, {}
+
+        def load_w1(pair):
+            w1_raw[pair] = sbuf("w1_raw%d" % pair, [P, PACK, K], F32)
+            nc.sync.dma_start(out=w1_raw[pair][:], in_=w1[2 * pair : 2 * pair + 2].rearrange("g (p j) k -> (g p) j k", j=PACK))
+            w1_bf[pair] = sbuf("w1_bf%d" % pair, [P, PACK, K // PACK, PACK], BF16)
+
+        def load_x(pair, c0, c1):
+            raw = sbuf("x_raw%d_%d" % (pair, c0), [P, PACK, (c1 - c0) * CHUNK], F32)
+            nc.sync.dma_start(
+                out=raw[:],
+                in_=x[2 * pair : 2 * pair + 2].rearrange("g (p j) n -> (g p) j n", j=PACK)[:, :, c0 * CHUNK : c1 * CHUNK],
+            )
+            for c in range(c0, c1):
+                x_raw[pair, c] = (raw, c - c0)
+
+        def load_w2(pair):
+            w2_raw[pair] = sbuf("w2_raw%d" % pair, [P, 2, PACK, M], F32)
+            nc.sync.dma_start(out=w2_raw[pair][:], in_=w2[2 * pair : 2 * pair + 2].rearrange("g (p j) m -> p g j m", j=PACK))
+            w2_bf[pair] = sbuf("w2_bf%d" % pair, [P, 2, M, PACK], BF16)
+
+        def load_r(pair):
+            r_sb[pair] = sbuf("r%d" % pair, [P, 2, N], F32)
+            nc.sync.dma_start(out=r_sb[pair][:], in_=r[2 * pair : 2 * pair + 2].rearrange("g m n -> m g n"))
+            res[pair] = sbuf("res%d" % pair, [P, 2, N], F32)
+
+        hs_sb = sbuf("hs", [P, G, 2 * PACK], F32)
+
+        def load_hs(queue):
+            queue.dma_start(out=hs_sb[:, :, 0:PACK], in_=hs.rearrange("g (p j) o -> p g (j o)", j=PACK))
+
+        def round_w1(engine, pair, s0, s1):
+            copy(
+                engine,
+                w1_bf[pair][:, :, s0:s1, :].rearrange("p t s j -> p s j t"),
+                w1_raw[pair][:].rearrange("p j (s t) -> p s j t", t=PACK)[:, s0:s1],
+            )
+
+        def quant_w1(pair):
+            w1_q[pair] = quantize("w1_%d" % pair, w1_bf[pair][:].rearrange("p t s j -> p (t s j)"))
+
+        def round_x(engine, pair, c0, c1):
+            raw, at = x_raw[pair, c0]
+            width = (c1 - c0) * CHUNK
+            x_bf[pair, c0] = sbuf("x_bf%d_%d" % (pair, c0), [P, width, PACK], BF16)
+            copy(
+                engine,
+                x_bf[pair, c0][:].rearrange("p (a i) j -> p a j i", i=4),
+                raw[:, :, at * CHUNK : at * CHUNK + width].rearrange("p j (a i) -> p a j i", i=4),
+            )
+
+        def quant_x(pair, c0, c1):
+            codes, scales = quantize("x%d_%d" % (pair, c0), x_bf[pair, c0][:].rearrange("p n j -> p (n j)"))
+            for c in range(c0, c1):
+                cols = slice((c - c0) * CHUNK, (c - c0 + 1) * CHUNK)
+                x_q[pair, c] = (codes, scales, cols)
+
+        def round_w2(engine, pair, c0, c1):
+            for c in range(c0, c1):
+                copy(
+                    engine,
+                    w2_bf[pair][:, c].rearrange("p (a i) j -> p a j i", i=4),
+                    w2_raw[pair][:, c].rearrange("p j (a i) -> p a j i", i=4),
+                )
+
+        def quant_w2(pair):
+            w2_q[pair] = quantize("w2_%d" % pair, w2_bf[pair][:].rearrange("p g m j -> p (g m j)"))
+
+        def layer1(u):
+            pair, chunk = divmod(u, CHUNKS)
+            w_codes, w_scales = w1_q[pair]
+            x_codes, x_scales, cols = x_q[pair, chunk]
+            for c in range(2):
+                rows = slice(c * ROWS, (c + 1) * ROWS)
+                for t in range(PACK):
+                    hidden = slice(t * P, (t + 1) * P)
+                    nc.tensor.matmul_mx(
+                        out=z_banks[c][u % Z_BANKS][:, t, :],
+                        lhsT=w_codes[rows, hidden].bitcast(FP8X4),
+                        lhsT_scale=w_scales[rows, hidden],
+                        rhs=x_codes[rows, cols].bitcast(FP8X4),
+                        rhs_scale=x_scales[rows, cols],
+                        start=True,
+                        stop=True,
+                    )
+
+        def sigmoid(u):
+            sig[u] = sbuf("sig%d" % u, [P, 2, CHUNK, PACK], F32)
+            for c in range(2):
+                nc.scalar.activation(
+                    out=sig[u][:, c], in_=z_banks[c][u % Z_BANKS][:].rearrange("p t n -> p n t"), func=SIGMOID
+                )
+
+        def scale(u):
+            pair = u // CHUNKS
+            h_bf[u] = sbuf("h_bf%d" % u, [P, 2, CHUNK, PACK], BF16)
+            nc.vector.tensor_tensor(
+                out=h_bf[u][:],
+                in0=sig[u][:],
+                in1=hs_sb[:, 2 * pair : 2 * pair + 2, 0:PACK].unsqueeze(2).to_broadcast([P, 2, CHUNK, PACK]),
+                op=MULT,
+            )
+
+        def quant_h(u):
+            h_q[u] = quantize("h%d" % u, h_bf[u][:].rearrange("p c n j -> p (c n j)"))
+
+        def layer2(u, bank):
+            w_codes, w_scales = w2_q[u // CHUNKS]
+            h_codes, h_scales = h_q[u]
+            half = slice((u % 2) * CHUNK, (u % 2 + 1) * CHUNK)
+            for c in range(2):
+                cols = slice(c * CHUNK, (c + 1) * CHUNK)
+                nc.tensor.matmul_mx(
+                    out=y_banks[bank][:, c, half],
+                    lhsT=w_codes[:, cols].bitcast(FP8X4),
+                    lhsT_scale=w_scales[:, cols],
+                    rhs=h_codes[:, cols].bitcast(FP8X4),
+                    rhs_scale=h_scales[:, cols],
+                    start=True,
+                    stop=True,
+                )
+
+        def residual(u0, u1, bank):
+            pair, chunk = divmod(u0, CHUNKS)
+            cols = slice(chunk * CHUNK, (chunk + u1 - u0) * CHUNK)
+            in_bank = slice((u0 % 2) * CHUNK, (u0 % 2 + u1 - u0) * CHUNK)
+            nc.vector.tensor_tensor(
+                out=res[pair][:, :, cols], in0=y_banks[bank][:, :, in_bank], in1=r_sb[pair][:, :, cols], op=ADD
+            )
+
+        def store(pair, c0, c1):
+            cols = slice(c0 * CHUNK, c1 * CHUNK)
+            nc.sync.dma_start(
+                out=out[2 * pair : 2 * pair + 2].rearrange("g m n -> m g n")[:, :, cols], in_=res[pair][:, :, cols]
+            )
+
+
+        load_w1(0)
+        load_x(0, 0, 2)
+        load_x(0, 2, 4)
+        load_hs(nc.sync)
+        load_w2(0)
+        load_x(1, 0, 2)
+        load_w1(1)
+        load_r(0)
+        load_x(1, 2, 4)
+        load_w2(1)
+        load_r(1)
+        round_w1("vector", 0, 0, 84)
+        round_w1("scalar", 0, 84, 128)
+        quant_w1(0)
+        round_x("scalar", 0, 0, 1)
+        quant_x(0, 0, 1)
+        layer1(0)
+        round_x("scalar", 0, 1, 2)
+        round_x("vector", 0, 2, 4)
+        quant_x(0, 1, 2)
+        layer1(1)
+        quant_x(0, 2, 4)
+        layer1(2)
+        sigmoid(0)
+        layer1(3)
+        round_w2("vector", 0, 0, 2)
+        sigmoid(1)
+        scale(0)
+        quant_w2(0)
+        round_x("scalar", 1, 0, 1)
+        quant_h(0)
+        scale(1)
+        sigmoid(2)
+        layer2(0, 0)
+        round_w1("vector", 1, 0, 48)
+        round_w1("scalar", 1, 48, 128)
+        quant_h(1)
+        layer2(1, 0)
+        scale(2)
+        quant_x(1, 0, 1)
+        quant_w1(1)
+        layer1(4)
+        sigmoid(3)
+        quant_h(2)
+        layer2(2, 1)
+        round_x("scalar", 1, 1, 2)
+        round_w2("scalar", 1, 0, 1)
+        scale(3)
+        quant_x(1, 1, 2)
+        layer1(5)
+        sigmoid(4)
+        residual(0, 2, 0)
+        quant_h(3)
+        layer2(3, 1)
+        round_x("scalar", 1, 2, 4)
+        scale(4)
+        quant_x(1, 2, 4)
+        layer1(6)
+        sigmoid(5)
+        layer1(7)
+        round_w2("scalar", 1, 1, 2)
+        residual(2, 4, 1)
+        store(0, 0, 4)
+        quant_h(4)
+        scale(5)
+        sigmoid(6)
+        quant_w2(1)
+        layer2(4, 0)
+        quant_h(5)
+        layer2(5, 0)
+        scale(6)
+        sigmoid(7)
+        scale(7)
+        quant_h(6)
+        layer2(6, 1)
+        quant_h(7)
+        layer2(7, 1)
+        residual(4, 6, 0)
+        store(1, 0, 2)
+        residual(6, 8, 1)
+        store(1, 2, 4)

@@ -52,6 +52,12 @@ def tile_rows_gmlp_sigmoid_res_kernel(tc, x, w1, hs, w2, r, out):
         w1_bf, w2_bf, x_bf, h_bf, sig, res = {}, {}, {}, {}, {}, {}
         w1_q, w2_q, x_q, h_q = {}, {}, {}, {}
 
+        def warm():
+            zero = sbuf("zero", [P, 1], F32)
+            unused = sbuf("unused", [P, 1], F32)
+            nc.gpsimd.memset(zero[:], 0.0)
+            nc.scalar.activation(out=unused[:], in_=zero[:], func=SIGMOID)
+
         def load_w1(pair):
             w1_raw[pair] = sbuf("w1_raw%d" % pair, [P, PACK, K], F32)
             nc.sync.dma_start(out=w1_raw[pair][:], in_=w1[2 * pair : 2 * pair + 2].rearrange("g (p j) k -> (g p) j k", j=PACK))
@@ -186,16 +192,15 @@ def tile_rows_gmlp_sigmoid_res_kernel(tc, x, w1, hs, w2, r, out):
                 out=out[2 * pair : 2 * pair + 2].rearrange("g m n -> m g n")[:, :, cols], in_=res[pair][:, :, cols]
             )
 
-
+        warm()
         load_w1(0)
         load_x(0, 0, 2)
         load_x(0, 2, 4)
-        load_hs(nc.sync)
         load_w2(0)
-        load_x(1, 0, 2)
+        load_hs(nc.sync)
         load_w1(1)
+        load_x(1, 0, 4)
         load_r(0)
-        load_x(1, 2, 4)
         load_w2(1)
         load_r(1)
         round_w1("vector", 0, 0, 84)
@@ -216,18 +221,18 @@ def tile_rows_gmlp_sigmoid_res_kernel(tc, x, w1, hs, w2, r, out):
         sigmoid(1)
         scale(0)
         quant_w2(0)
-        round_x("scalar", 1, 0, 1)
         quant_h(0)
         scale(1)
         sigmoid(2)
         layer2(0, 0)
         round_w1("vector", 1, 0, 48)
         round_w1("scalar", 1, 48, 128)
+        round_x("scalar", 1, 0, 1)
         quant_h(1)
         layer2(1, 0)
         scale(2)
-        quant_x(1, 0, 1)
         quant_w1(1)
+        quant_x(1, 0, 1)
         layer1(4)
         sigmoid(3)
         quant_h(2)

from contextlib import ExitStack

import concourse.mybir as mybir

G, D, K, M, N = 4, 256, 512, 128, 512
FLOPS = 2 * G * N * (D * K + K * M)

F32 = mybir.dt.float32
BF16 = mybir.dt.bfloat16
U32 = mybir.dt.uint32
U8 = mybir.dt.uint8
FP8X4 = mybir.dt.float8_e4m3fn_x4
SIGMOID = mybir.ActivationFunctionType.Sigmoid
MULT = mybir.AluOpType.mult
ADD = mybir.AluOpType.add

P = 128
PACK = 4
ROWS = 64
CHUNK = 128
CHUNKS = N // CHUNK
Z_BANKS = 3


def tile_rows_gmlp_sigmoid_res_kernel(tc, x, w1, hs, w2, r, out):
    nc = tc.nc
    with ExitStack() as ctx:
        sb = ctx.enter_context(tc.tile_pool(name="sb", bufs=1))
        ps = ctx.enter_context(tc.psum_pool(name="ps", bufs=1))
        ctx.enter_context(tc.manual_schedule())

        def sbuf(name, shape, dtype):
            return sb.tile(shape, dtype, name=name, align_bytes=64)

        z_banks = [[ps.tile([P, PACK, CHUNK], F32, name="z%d_%d" % (c, i)) for i in range(Z_BANKS)] for c in range(2)]
        y_banks = [ps.tile([P, 2, 2 * CHUNK], F32, name="y%d" % i) for i in range(2)]

        def copy(engine, dst, src):
            if engine == "vector":
                nc.vector.tensor_copy(out=dst, in_=src)
            else:
                nc.scalar.copy(out=dst, in_=src)

        def quantize(name, values):
            words = values.shape[1] // PACK
            codes = sbuf(name + "_codes", [P, words], U32)
            scales = sbuf(name + "_scales", [P, words], U8)
            nc.vector.quantize_mx(out=codes[:].bitcast(FP8X4), scales=scales[:], in_=values)
            return codes, scales

        x_raw, w1_raw, w2_raw, r_sb = {}, {}, {}, {}
        w1_bf, w2_bf, x_bf, h_bf, sig, res = {}, {}, {}, {}, {}, {}
        w1_q, w2_q, x_q, h_q = {}, {}, {}, {}

        def warm():
            zero = sbuf("zero", [P, 1], F32)
            unused = sbuf("unused", [P, 1], F32)
            nc.gpsimd.memset(zero[:], 0.0)
            nc.scalar.activation(out=unused[:], in_=zero[:], func=SIGMOID)

        def load_w1(pair):
            w1_raw[pair] = sbuf("w1_raw%d" % pair, [P, PACK, K], F32)
            nc.sync.dma_start(out=w1_raw[pair][:], in_=w1[2 * pair : 2 * pair + 2].rearrange("g (p j) k -> (g p) j k", j=PACK))
            w1_bf[pair] = sbuf("w1_bf%d" % pair, [P, PACK, K // PACK, PACK], BF16)

        def load_x(pair, c0, c1):
            raw = sbuf("x_raw%d_%d" % (pair, c0), [P, PACK, (c1 - c0) * CHUNK], F32)
            nc.sync.dma_start(
                out=raw[:],
                in_=x[2 * pair : 2 * pair + 2].rearrange("g (p j) n -> (g p) j n", j=PACK)[:, :, c0 * CHUNK : c1 * CHUNK],
            )
            for c in range(c0, c1):
                x_raw[pair, c] = (raw, c - c0)

        def load_w2(pair):
            w2_raw[pair] = sbuf("w2_raw%d" % pair, [P, 2, PACK, M], F32)
            nc.sync.dma_start(out=w2_raw[pair][:], in_=w2[2 * pair : 2 * pair + 2].rearrange("g (p j) m -> p g j m", j=PACK))
            w2_bf[pair] = sbuf("w2_bf%d" % pair, [P, 2, M, PACK], BF16)

        def load_r(pair):
            r_sb[pair] = sbuf("r%d" % pair, [P, 2, N], F32)
            nc.sync.dma_start(out=r_sb[pair][:], in_=r[2 * pair : 2 * pair + 2].rearrange("g m n -> m g n"))
            res[pair] = sbuf("res%d" % pair, [P, 2, N], F32)

        hs_sb = sbuf("hs", [P, G, 2 * PACK], F32)

        def load_hs(queue):
            queue.dma_start(out=hs_sb[:, :, 0:PACK], in_=hs.rearrange("g (p j) o -> p g (j o)", j=PACK))

        def round_w1(engine, pair, s0, s1):
            copy(
                engine,
                w1_bf[pair][:, :, s0:s1, :].rearrange("p t s j -> p s j t"),
                w1_raw[pair][:].rearrange("p j (s t) -> p s j t", t=PACK)[:, s0:s1],
            )

        def quant_w1(pair):
            w1_q[pair] = quantize("w1_%d" % pair, w1_bf[pair][:].rearrange("p t s j -> p (t s j)"))

        def round_x(engine, pair, c0, c1):
            raw, at = x_raw[pair, c0]
            width = (c1 - c0) * CHUNK
            x_bf[pair, c0] = sbuf("x_bf%d_%d" % (pair, c0), [P, width, PACK], BF16)
            copy(
                engine,
                x_bf[pair, c0][:].rearrange("p (a i) j -> p a j i", i=4),
                raw[:, :, at * CHUNK : at * CHUNK + width].rearrange("p j (a i) -> p a j i", i=4),
            )

        def quant_x(pair, c0, c1):
            codes, scales = quantize("x%d_%d" % (pair, c0), x_bf[pair, c0][:].rearrange("p n j -> p (n j)"))
            for c in range(c0, c1):
                cols = slice((c - c0) * CHUNK, (c - c0 + 1) * CHUNK)
                x_q[pair, c] = (codes, scales, cols)

        def round_w2(engine, pair, c0, c1):
            for c in range(c0, c1):
                copy(
                    engine,
                    w2_bf[pair][:, c].rearrange("p (a i) j -> p a j i", i=4),
                    w2_raw[pair][:, c].rearrange("p j (a i) -> p a j i", i=4),
                )

        def quant_w2(pair):
            w2_q[pair] = quantize("w2_%d" % pair, w2_bf[pair][:].rearrange("p g m j -> p (g m j)"))

        def layer1(u):
            pair, chunk = divmod(u, CHUNKS)
            w_codes, w_scales = w1_q[pair]
            x_codes, x_scales, cols = x_q[pair, chunk]
            for c in range(2):
                rows = slice(c * ROWS, (c + 1) * ROWS)
                for t in range(PACK):
                    hidden = slice(t * P, (t + 1) * P)
                    nc.tensor.matmul_mx(
                        out=z_banks[c][u % Z_BANKS][:, t, :],
                        lhsT=w_codes[rows, hidden].bitcast(FP8X4),
                        lhsT_scale=w_scales[rows, hidden],
                        rhs=x_codes[rows, cols].bitcast(FP8X4),
                        rhs_scale=x_scales[rows, cols],
                        start=True,
                        stop=True,
                    )

        def sigmoid(u):
            sig[u] = sbuf("sig%d" % u, [P, 2, CHUNK, PACK], F32)
            for c in range(2):
                nc.scalar.activation(
                    out=sig[u][:, c], in_=z_banks[c][u % Z_BANKS][:].rearrange("p t n -> p n t"), func=SIGMOID
                )

        def scale(u):
            pair = u // CHUNKS
            h_bf[u] = sbuf("h_bf%d" % u, [P, 2, CHUNK, PACK], BF16)
            nc.vector.tensor_tensor(
                out=h_bf[u][:],
                in0=sig[u][:],
                in1=hs_sb[:, 2 * pair : 2 * pair + 2, 0:PACK].unsqueeze(2).to_broadcast([P, 2, CHUNK, PACK]),
                op=MULT,
            )

        def quant_h(u):
            h_q[u] = quantize("h%d" % u, h_bf[u][:].rearrange("p c n j -> p (c n j)"))

        def layer2(u, bank):
            w_codes, w_scales = w2_q[u // CHUNKS]
            h_codes, h_scales = h_q[u]
            half = slice((u % 2) * CHUNK, (u % 2 + 1) * CHUNK)
            for c in range(2):
                cols = slice(c * CHUNK, (c + 1) * CHUNK)
                nc.tensor.matmul_mx(
                    out=y_banks[bank][:, c, half],
                    lhsT=w_codes[:, cols].bitcast(FP8X4),
                    lhsT_scale=w_scales[:, cols],
                    rhs=h_codes[:, cols].bitcast(FP8X4),
                    rhs_scale=h_scales[:, cols],
                    start=True,
                    stop=True,
                )

        def residual(u0, u1, bank):
            pair, chunk = divmod(u0, CHUNKS)
            cols = slice(chunk * CHUNK, (chunk + u1 - u0) * CHUNK)
            in_bank = slice((u0 % 2) * CHUNK, (u0 % 2 + u1 - u0) * CHUNK)
            nc.vector.tensor_tensor(
                out=res[pair][:, :, cols], in0=y_banks[bank][:, :, in_bank], in1=r_sb[pair][:, :, cols], op=ADD
            )

        def store(pair, c0, c1):
            cols = slice(c0 * CHUNK, c1 * CHUNK)
            nc.sync.dma_start(
                out=out[2 * pair : 2 * pair + 2].rearrange("g m n -> m g n")[:, :, cols], in_=res[pair][:, :, cols]
            )

        warm()
        load_w1(0)
        load_x(0, 0, 2)
        load_x(0, 2, 4)
        load_w2(0)
        load_hs(nc.sync)
        load_w1(1)
        load_x(1, 0, 4)
        load_r(0)
        load_w2(1)
        load_r(1)
        round_w1("vector", 0, 0, 84)
        round_w1("scalar", 0, 84, 128)
        quant_w1(0)
        round_x("scalar", 0, 0, 1)
        quant_x(0, 0, 1)
        layer1(0)
        round_x("scalar", 0, 1, 2)
        round_x("vector", 0, 2, 4)
        quant_x(0, 1, 2)
        layer1(1)
        quant_x(0, 2, 4)
        layer1(2)
        sigmoid(0)
        layer1(3)
        round_w2("vector", 0, 0, 2)
        sigmoid(1)
        scale(0)
        quant_w2(0)
        quant_h(0)
        scale(1)
        sigmoid(2)
        layer2(0, 0)
        round_w1("vector", 1, 0, 48)
        round_w1("scalar", 1, 48, 128)
        round_x("scalar", 1, 0, 1)
        quant_h(1)
        layer2(1, 0)
        scale(2)
        quant_w1(1)
        quant_x(1, 0, 1)
        layer1(4)
        sigmoid(3)
        quant_h(2)
        layer2(2, 1)
        round_x("scalar", 1, 1, 2)
        round_w2("scalar", 1, 0, 1)
        scale(3)
        quant_x(1, 1, 2)
        layer1(5)
        sigmoid(4)
        residual(0, 2, 0)
        quant_h(3)
        layer2(3, 1)
        round_x("scalar", 1, 2, 4)
        scale(4)
        quant_x(1, 2, 4)
        layer1(6)
        sigmoid(5)
        layer1(7)
        round_w2("scalar", 1, 1, 2)
        residual(2, 4, 1)
        store(0, 0, 4)
        quant_h(4)
        scale(5)
        sigmoid(6)
        quant_w2(1)
        layer2(4, 0)
        quant_h(5)
        layer2(5, 0)
        scale(6)
        sigmoid(7)
        scale(7)
        quant_h(6)
        layer2(6, 1)
        quant_h(7)
        layer2(7, 1)
        residual(4, 6, 0)
        store(1, 0, 2)
        residual(6, 8, 1)
        store(1, 2, 4)
